import numpy as np
import ml_dtypes


def mxq(x, axis, fmt="e4m3"):
    dtype, down = {"e4m3": (ml_dtypes.float8_e4m3fn, 7), "e5m2": (ml_dtypes.float8_e5m2, 14)}[fmt]
    v = np.moveaxis(np.asarray(x, np.float32).astype(ml_dtypes.bfloat16).astype(np.float64), axis, -1)
    blocks = v.reshape(v.shape[:-1] + (-1, 32))
    amax = np.abs(blocks).max(-1, keepdims=True)
    byte = np.maximum(np.where(amax > 0, np.frexp(amax)[1] - 1 + 127, 0) - down, 1)
    scale = np.exp2(byte - 127.0)
    codes = (blocks / scale).astype(np.float32).astype(dtype).astype(np.float64)
    return np.moveaxis((codes * scale).reshape(v.shape), -1, axis)


WIDE = False


def mx_kscale(k, group=512):
    if not WIDE:
        return np.ones(k)
    levels = np.array([10, -10, 5, -5, 0])
    if group != 512:
        return np.exp2(np.random.permutation(np.resize(levels, k // group))).repeat(group)
    if k % 512:
        return np.exp2(np.random.permutation(np.resize(levels, k // 32))).repeat(32)
    a = np.empty((k // 512, 16))
    for p in range(k // 512):
        a[p, :8] = np.random.permutation(np.resize(levels, 8))
        for g in range(8):
            far = levels[np.abs(levels - a[p, g]) >= 10]
            a[p, g + 8] = far[np.random.randint(len(far))]
    return np.exp2(a.ravel()).repeat(32)


def f64(x):
    return np.asarray(x).astype(np.float64)


E2M1 = np.array([0.0, 0.5, 1.0, 1.5, 2.0, 3.0, 4.0, 6.0, -0.0, -0.5, -1.0, -1.5, -2.0, -3.0, -4.0, -6.0])


def pack_group(w):
    k, n = w.shape
    w = f64(np.asarray(w, np.float32).astype(ml_dtypes.bfloat16)).reshape(k // 32, 32, n)
    amax = np.abs(w).max(1)
    mant, ex = np.frexp(amax / 6.0)
    byte = np.clip(np.where(amax > 0, np.where(mant > 0.5, ex, ex - 1) + 127, 1), 1, 254)
    scaled = (w * np.exp2(127.0 - byte)[:, None, :]).reshape(k, n).astype(np.float32)
    c = np.ascontiguousarray(scaled.reshape(k // 4, 4, n).transpose(0, 2, 1)).astype(ml_dtypes.float4_e2m1fn).view(np.uint8) & 0xF
    return np.ascontiguousarray((c[..., 0::2] | (c[..., 1::2] << 4)).reshape(k // 4, 2 * n)), byte.astype(np.uint8)


def unpack_group(words, scales):
    p, n = words.shape[0], scales.shape[1]
    words = np.ascontiguousarray(words).reshape(p, n, 2)
    nib = np.empty((p, n, 4), np.uint8)
    nib[..., 0::2] = words & 0xF
    nib[..., 1::2] = words >> 4
    return E2M1[nib].transpose(0, 2, 1).reshape(4 * p, n) * np.repeat(np.exp2(scales.astype(np.float64) - 127.0), 32, axis=0)


def softplus(v):
    return np.log(1.0 + np.exp(v))


def sigmoid(v):
    return 1.0 / (1.0 + np.exp(-v))


G, D, M, O, N = 2, 256, 256, 256, 512


def setup_inputs():
    n = np.random.standard_normal
    s_d = mx_kscale(D, 0)
    s_o = mx_kscale(O, 0)
    w1_ = [pack_group(w) for w in n((G, D, M)) / np.sqrt(D) / s_d[:, None]]
    w2_ = [pack_group(w) for w in n((G, D, M)) / np.sqrt(D) / s_d[:, None]]
    wo_ = [pack_group(w) for w in n((G, O, M)) / np.sqrt(O) / s_o[:, None]]
    return {
        "x": (n((G, D, N)) * s_d[:, None]).astype(np.float32),
        "w1_words": np.stack([w[0] for w in w1_]),
        "w1_scales": np.stack([w[1] for w in w1_]),
        "w2_words": np.stack([w[0] for w in w2_]),
        "w2_scales": np.stack([w[1] for w in w2_]),
        "gn": (np.random.uniform(0.5, 2.0, (G, M, 1))).astype(np.float32),
        "wo_words": np.stack([w[0] for w in wo_]),
        "wo_scales": np.stack([w[1] for w in wo_]),
        "dy": (n((G, O, N)) * s_o[:, None]).astype(np.float32),
        "old": (0.3 * n((G, M, N))).astype(np.float32),
    }


def reference(x, w1_words, w1_scales, w2_words, w2_scales, gn, wo_words, wo_scales, dy, old):
    w1 = np.stack([unpack_group(w1_words[g], w1_scales[g]) for g in range(G)])
    xq = mxq(f64(x), 1, "e4m3")
    z1 = w1.transpose(0, 2, 1) @ xq
    w2 = np.stack([unpack_group(w2_words[g], w2_scales[g]) for g in range(G)])
    z2 = w2.transpose(0, 2, 1) @ xq
    sp = softplus(z1) * softplus(z2)
    wo = np.stack([unpack_group(wo_words[g], wo_scales[g]) for g in range(G)])
    dyq = mxq(f64(dy), 1, "e4m3")
    c0 = wo.transpose(0, 2, 1) @ dyq
    dsp = c0 * sigmoid(z1 - z2) / (sp * f64(gn) + 1.0) * f64(gn)
    dz1 = c0 * np.log(sp * f64(gn) + 1.0) * sigmoid(z1 - z2) * (1.0 - sigmoid(z1 - z2)) + dsp * softplus(z2) * sigmoid(z1)
    y = dz1 + f64(old)
    return y

@@ -1,0 +1,222 @@
+from contextlib import ExitStack
+
+import concourse.mybir as mybir
+
+F32 = mybir.dt.float32
+BF16 = mybir.dt.bfloat16
+I32 = mybir.dt.int32
+U32 = mybir.dt.uint32
+U8 = mybir.dt.uint8
+FP8X4 = mybir.dt.float8_e4m3fn_x4
+FP4X4 = mybir.dt.float4_e2m1fn_x4
+ACT = mybir.ActivationFunctionType
+ALU = mybir.AluOpType
+
+G, D, M, N = 2, 256, 256, 512
+P = 128
+PACK = 4
+ROWS = D // PACK
+HALVES = M // P
+TILES = G * HALVES
+CHUNKS = 2
+CW = N // CHUNKS
+TINY = 2.0**-60
+FLOPS = 3 * 2 * G * D * M * N
+
+
+def tile_rows_bsoftprod_kernel(tc, x, w1_words, w1_scales, w2_words, w2_scales, gn, wo_words, wo_scales, dy, old, out):
+    nc = tc.nc
+    with ExitStack() as ctx:
+        sb = ctx.enter_context(tc.tile_pool(name="sb", bufs=1))
+        ps = ctx.enter_context(tc.psum_pool(name="ps", bufs=1))
+        ctx.enter_context(tc.manual_schedule())
+
+        def cols(t):
+            return slice(t * N, (t + 1) * N)
+
+        def wide(name):
+            return sb.tile([P, TILES * N], F32, name=name, align_bytes=64)
+
+        words = {}
+        planes = {}
+        for name in ("w1", "w2", "wo"):
+            words[name] = sb.tile([P, 2 * M], U8, name=name + "_words", align_bytes=64)
+            planes[name] = sb.tile([P, M], U8, name=name + "_plane", align_bytes=64)
+            nc.vector.memset(planes[name][:].bitcast(U32), 0)
+
+        def load_words(name, src):
+            nc.sync.dma_start(out=words[name][:].bitcast(I32), in_=src.rearrange("g p b -> (g p) b").bitcast(I32))
+
+        def load_plane(name, src, q):
+            rows = src.rearrange("g f m -> (g f) m")
+            nc.sync.dma_start(out=planes[name][32 * q : 32 * q + 4, :].bitcast(I32), in_=rows[4 * q : 4 * q + 4, :].bitcast(I32))
+
+        def load_raw(name, src, c):
+            raw = sb.tile([P, PACK, CW], F32, name="%s_raw%d" % (name, c), align_bytes=64)
+            nc.sync.dma_start(out=raw[:], in_=src.rearrange("g (p j) n -> (g p) j n", j=PACK)[:, :, c * CW : (c + 1) * CW])
+            return raw
+
+        def interleave(name, raw, c):
+            grouped = sb.tile([P, CW, PACK], BF16, name="%s_bf%d" % (name, c), align_bytes=64)
+            nc.vector.tensor_copy(
+                out=grouped[:].rearrange("p (c i) j -> p c j i", i=4),
+                in_=raw[:].rearrange("p j (c i) -> p c j i", i=4),
+            )
+            return grouped
+
+        def quantize(codes, scales, grouped, c):
+            window = slice(c * CW, (c + 1) * CW)
+            nc.vector.quantize_mx(
+                out=codes[:, window].bitcast(FP8X4),
+                scales=scales[:, window],
+                in_=grouped[:].rearrange("p n j -> p (n j)"),
+            )
+
+        def product(name, codes, scales, t, slot):
+            g, h = divmod(t, HALVES)
+            rows = slice(g * ROWS, (g + 1) * ROWS)
+            bank = ps.tile([P, N], F32, name="bank%d_%d" % (g, slot))
+            nc.tensor.matmul_mx(
+                out=bank[:],
+                lhsT=words[name][rows, 2 * P * h : 2 * P * (h + 1)].bitcast(FP4X4),
+                lhsT_scale=planes[name][rows, P * h : P * (h + 1)],
+                rhs=codes[rows, :].bitcast(FP8X4),
+                rhs_scale=scales[rows, :],
+                start=True,
+                stop=True,
+            )
+            return bank
+
+        x_raw = [load_raw("x", x, c) for c in range(CHUNKS)]
+        weights = (("w1", w1_words, w1_scales), ("w2", w2_words, w2_scales))
+        for name, src_words, src_scales in weights:
+            load_words(name, src_words)
+            for q in (0, 1):
+                load_plane(name, src_scales, q)
+        dy_raw = [load_raw("dy", dy, 0)]
+        for name, src_words, src_scales in weights:
+            for q in (2, 3):
+                load_plane(name, src_scales, q)
+        dy_raw.append(load_raw("dy", dy, 1))
+        gain = sb.tile([P, TILES], F32, name="gain")
+        with nc.allow_non_contiguous_dma(reason="one gain a partition"):
+            nc.sync.dma_start(out=gain[:], in_=gn.rearrange("g (h p) o -> p (g h o)", p=P))
+        load_words("wo", wo_words)
+        for q in range(4):
+            load_plane("wo", wo_scales, q)
+        old_sb = wide("old_sb")
+        nc.sync.dma_start(out=old_sb[:].rearrange("p (t n) -> p t n", n=N), in_=old.rearrange("g (h p) n -> p (g h) n", p=P))
+
+        x_codes = sb.tile([P, N], U32, name="x_codes", align_bytes=64)
+        x_scales = sb.tile([P, N], U8, name="x_scales", align_bytes=64)
+        dy_codes = sb.tile([P, N], U32, name="dy_codes", align_bytes=64)
+        dy_scales = sb.tile([P, N], U8, name="dy_scales", align_bytes=64)
+        for c in range(CHUNKS):
+            quantize(x_codes, x_scales, interleave("x", x_raw[c], c), c)
+
+        z1, z2 = [], []
+        for t in range(TILES):
+            h = t % HALVES
+            z1.append(product("w1", x_codes, x_scales, t, 2 * h))
+            z2.append(product("w2", x_codes, x_scales, t, 2 * h + 1))
+
+        m1, m2, z2_sb, diff, sd, hh = (wide(n) for n in ("m1", "m2", "z2_sb", "diff", "sd", "hh"))
+        l1, l2, s1, s2, prod, lnq = (wide(n) for n in ("l1", "l2", "s1", "s2", "prod", "lnq"))
+        sq, aa, bb, rq, ww, yy = (wide(n) for n in ("sq", "aa", "bb", "rq", "ww", "yy"))
+
+        def act(dst, src, func, **kw):
+            nc.scalar.activation(out=dst, in_=src, func=func, **kw)
+
+        def stt(dst, in0, scalar, op0, in1, op1):
+            nc.vector.scalar_tensor_tensor(out=dst, in0=in0, scalar=scalar, in1=in1, op0=op0, op1=op1)
+
+        def tt(dst, in0, in1, op):
+            nc.vector.tensor_tensor(out=dst, in0=in0, in1=in1, op=op)
+
+        def sig_d(t):
+            act(sd[:, cols(t)], diff[:, cols(t)], ACT.Sigmoid)
+
+        def h_step(t):
+            stt(hh[:, cols(t)], m1[:, cols(t)], 1.0, ALU.subtract, sd[:, cols(t)], ALU.mult)
+
+        def d_step(t):
+            tt(diff[:, cols(t)], z1[t][:], z2_sb[:, cols(t)], ALU.subtract)
+
+        quantize(dy_codes, dy_scales, interleave("dy", dy_raw[0], 0), 0)
+        for t in range(TILES):
+            act(m1[:, cols(t)], z1[t][:], ACT.Sigmoid, scale=-1.0)
+            act(m2[:, cols(t)], z2[t][:], ACT.Sigmoid, scale=-1.0)
+            nc.vector.tensor_copy(out=z2_sb[:, cols(t)], in_=z2[t][:])
+            if t == 0:
+                dy_last = interleave("dy", dy_raw[1], 1)
+            else:
+                d_step(t - 1)
+        quantize(dy_codes, dy_scales, dy_last, 1)
+        d_step(TILES - 1)
+        for t in range(TILES):
+            sig_d(t)
+            h_step(t)
+
+        c0 = []
+
+        def ln_q(t):
+            act(lnq[:, cols(t)], prod[:, cols(t)], ACT.Ln, scale=gain[:, t : t + 1], bias=1.0)
+
+        def square(t):
+            act(sq[:, cols(t)], sd[:, cols(t)], ACT.Square, bias=-0.5)
+
+        def p_step(t):
+            tt(prod[:, cols(t)], s1[:, cols(t)], s2[:, cols(t)], ALU.mult)
+
+        def b_step(t):
+            stt(bb[:, cols(t)], hh[:, cols(t)], gain[:, t : t + 1], ALU.mult, s2[:, cols(t)], ALU.mult)
+
+        def a_step(t):
+            stt(aa[:, cols(t)], sq[:, cols(t)], 0.25, ALU.subtract, lnq[:, cols(t)], ALU.mult)
+
+        for t in range(TILES):
+            act(l1[:, cols(t)], m1[:, cols(t)], ACT.Ln, bias=TINY)
+            act(l2[:, cols(t)], m2[:, cols(t)], ACT.Ln, bias=TINY)
+            stt(s1[:, cols(t)], z1[t][:], -1.0, ALU.mult, l1[:, cols(t)], ALU.min)
+            c0.append(product("wo", dy_codes, dy_scales, t, 2 * (t % HALVES)))
+            if t >= 1:
+                p_step(t - 1)
+            stt(s2[:, cols(t)], z2[t][:], -1.0, ALU.mult, l2[:, cols(t)], ALU.min)
+        b_step(0)
+        p_step(TILES - 1)
+        ln_q(0)
+        ln_q(1)
+        square(0)
+        square(1)
+        ln_q(2)
+        square(2)
+        ln_q(3)
+        for t in range(TILES - 1):
+            b_step(t + 1)
+            a_step(t)
+
+        for t in range(TILES):
+            act(rq[:, cols(t)], lnq[:, cols(t)], ACT.Exp, scale=-1.0)
+            if t == 1:
+                square(3)
+
+        def br_step(t):
+            tt(bb[:, cols(t)], bb[:, cols(t)], rq[:, cols(t)], ALU.mult)
+
+        def w_step(t):
+            tt(ww[:, cols(t)], bb[:, cols(t)], aa[:, cols(t)], ALU.subtract)
+
+        def cw_step(t):
+            tt(ww[:, cols(t)], c0[t][:], ww[:, cols(t)], ALU.mult)
+
+        def y_step(t):
+            g, h = divmod(t, HALVES)
+            tt(yy[:, cols(t)], ww[:, cols(t)], old_sb[:, cols(t)], ALU.add)
+            nc.sync.dma_start(out=out[g, h * P : (h + 1) * P, :], in_=yy[:, cols(t)])
+
+        for pair in ((0, 1), (2, 3)):
+            if pair[0] == 2:
+                a_step(3)
+            for step in (br_step, w_step, cw_step, y_step):
+                for t in pair:
+                    step(t)

@@ -20,6 +20,7 @@ HALVES = M // P
 TILES = G * HALVES
 CHUNKS = 2
 CW = N // CHUNKS
+POOL_COLS = 2 * N + 192
 TINY = 2.0**-60
 FLOPS = 3 * 2 * G * D * M * N
 
@@ -42,14 +43,15 @@ def tile_rows_bsoftprod_kernel(tc, x, w1_words, w1_scales, w2_words, w2_scales, 
         for name in ("w1", "w2", "wo"):
             words[name] = sb.tile([P, 2 * M], U8, name=name + "_words", align_bytes=64)
             planes[name] = sb.tile([P, M], U8, name=name + "_plane", align_bytes=64)
-            nc.vector.memset(planes[name][:].bitcast(U32), 0)
+            engine = nc.vector if name == "wo" else nc.gpsimd
+            engine.memset(planes[name][:].bitcast(U32), 0)
 
         def load_words(name, src):
             nc.sync.dma_start(out=words[name][:].bitcast(I32), in_=src.rearrange("g p b -> (g p) b").bitcast(I32))
 
-        def load_plane(name, src, q):
+        def load_plane(name, src, q, queue):
             rows = src.rearrange("g f m -> (g f) m")
-            nc.sync.dma_start(out=planes[name][32 * q : 32 * q + 4, :].bitcast(I32), in_=rows[4 * q : 4 * q + 4, :].bitcast(I32))
+            queue.dma_start(out=planes[name][32 * q : 32 * q + 4, :].bitcast(I32), in_=rows[4 * q : 4 * q + 4, :].bitcast(I32))
 
         def load_raw(name, src, c):
             raw = sb.tile([P, PACK, CW], F32, name="%s_raw%d" % (name, c), align_bytes=64)
@@ -92,18 +94,17 @@ def tile_rows_bsoftprod_kernel(tc, x, w1_words, w1_scales, w2_words, w2_scales, 
         for name, src_words, src_scales in weights:
             load_words(name, src_words)
             for q in (0, 1):
-                load_plane(name, src_scales, q)
-        dy_raw = [load_raw("dy", dy, 0)]
+                load_plane(name, src_scales, q, nc.sync)
         for name, src_words, src_scales in weights:
             for q in (2, 3):
-                load_plane(name, src_scales, q)
-        dy_raw.append(load_raw("dy", dy, 1))
+                load_plane(name, src_scales, q, nc.gpsimd)
+        dy_raw = [load_raw("dy", dy, c) for c in range(CHUNKS)]
+        load_words("wo", wo_words)
+        for q in range(4):
+            load_plane("wo", wo_scales, q, nc.sync)
         gain = sb.tile([P, TILES], F32, name="gain")
         with nc.allow_non_contiguous_dma(reason="one gain a partition"):
             nc.sync.dma_start(out=gain[:], in_=gn.rearrange("g (h p) o -> p (g h o)", p=P))
-        load_words("wo", wo_words)
-        for q in range(4):
-            load_plane("wo", wo_scales, q)
         old_sb = wide("old_sb")
         nc.sync.dma_start(out=old_sb[:].rearrange("p (t n) -> p t n", n=N), in_=old.rearrange("g (h p) n -> p (g h) n", p=P))
 
@@ -120,9 +121,9 @@ def tile_rows_bsoftprod_kernel(tc, x, w1_words, w1_scales, w2_words, w2_scales, 
             z1.append(product("w1", x_codes, x_scales, t, 2 * h))
             z2.append(product("w2", x_codes, x_scales, t, 2 * h + 1))
 
-        m1, m2, z2_sb, diff, sd, hh = (wide(n) for n in ("m1", "m2", "z2_sb", "diff", "sd", "hh"))
+        m1, m2, z2_sb, diff, sd, cs = (wide(n) for n in ("m1", "m2", "z2_sb", "diff", "sd", "cs"))
         l1, l2, s1, s2, prod, lnq = (wide(n) for n in ("l1", "l2", "s1", "s2", "prod", "lnq"))
-        sq, aa, bb, rq, ww, yy = (wide(n) for n in ("sq", "aa", "bb", "rq", "ww", "yy"))
+        t1, t2, rq, ww, yy = (wide(n) for n in ("t1", "t2", "rq", "ww", "yy"))
 
         def act(dst, src, func, **kw):
             nc.scalar.activation(out=dst, in_=src, func=func, **kw)
@@ -133,81 +134,63 @@ def tile_rows_bsoftprod_kernel(tc, x, w1_words, w1_scales, w2_words, w2_scales, 
         def tt(dst, in0, in1, op):
             nc.vector.tensor_tensor(out=dst, in0=in0, in1=in1, op=op)
 
-        def sig_d(t):
-            act(sd[:, cols(t)], diff[:, cols(t)], ACT.Sigmoid)
-
-        def h_step(t):
-            stt(hh[:, cols(t)], m1[:, cols(t)], 1.0, ALU.subtract, sd[:, cols(t)], ALU.mult)
-
         def d_step(t):
             tt(diff[:, cols(t)], z1[t][:], z2_sb[:, cols(t)], ALU.subtract)
 
         quantize(dy_codes, dy_scales, interleave("dy", dy_raw[0], 0), 0)
+        dy_last = interleave("dy", dy_raw[1], 1)
         for t in range(TILES):
             act(m1[:, cols(t)], z1[t][:], ACT.Sigmoid, scale=-1.0)
             act(m2[:, cols(t)], z2[t][:], ACT.Sigmoid, scale=-1.0)
             nc.vector.tensor_copy(out=z2_sb[:, cols(t)], in_=z2[t][:])
             if t == 0:
-                dy_last = interleave("dy", dy_raw[1], 1)
+                quantize(dy_codes, dy_scales, dy_last, 1)
             else:
                 d_step(t - 1)
-        quantize(dy_codes, dy_scales, dy_last, 1)
         d_step(TILES - 1)
+        c0 = [product("wo", dy_codes, dy_scales, t, 2 * (t % HALVES) + 1) for t in range(TILES)]
+        z2 = []
         for t in range(TILES):
-            sig_d(t)
-            h_step(t)
+            act(sd[:, cols(t)], diff[:, cols(t)], ACT.Sigmoid)
+            tt(cs[:, cols(t)], c0[t][:], sd[:, cols(t)], ALU.mult)
+            z2.append(product("w2", x_codes, x_scales, t, 2 * (t % HALVES) + 1))
 
-        c0 = []
+        def p_step(engine, lo, hi):
+            engine.tensor_tensor(out=prod[:, lo:hi], in0=s1[:, lo:hi], in1=s2[:, lo:hi], op=ALU.mult)
 
-        def ln_q(t):
-            act(lnq[:, cols(t)], prod[:, cols(t)], ACT.Ln, scale=gain[:, t : t + 1], bias=1.0)
+        def t2_step(t):
+            stt(t2[:, cols(t)], m1[:, cols(t)], 1.0, ALU.subtract, s2[:, cols(t)], ALU.mult)
 
-        def square(t):
-            act(sq[:, cols(t)], sd[:, cols(t)], ACT.Square, bias=-0.5)
-
-        def p_step(t):
-            tt(prod[:, cols(t)], s1[:, cols(t)], s2[:, cols(t)], ALU.mult)
-
-        def b_step(t):
-            stt(bb[:, cols(t)], hh[:, cols(t)], gain[:, t : t + 1], ALU.mult, s2[:, cols(t)], ALU.mult)
-
-        def a_step(t):
-            stt(aa[:, cols(t)], sq[:, cols(t)], 0.25, ALU.subtract, lnq[:, cols(t)], ALU.mult)
+        def t1_step(t):
+            stt(t1[:, cols(t)], sd[:, cols(t)], 1.0, ALU.subtract, lnq[:, cols(t)], ALU.mult)
 
         for t in range(TILES):
             act(l1[:, cols(t)], m1[:, cols(t)], ACT.Ln, bias=TINY)
             act(l2[:, cols(t)], m2[:, cols(t)], ACT.Ln, bias=TINY)
             stt(s1[:, cols(t)], z1[t][:], -1.0, ALU.mult, l1[:, cols(t)], ALU.min)
-            c0.append(product("wo", dy_codes, dy_scales, t, 2 * (t % HALVES)))
-            if t >= 1:
-                p_step(t - 1)
             stt(s2[:, cols(t)], z2[t][:], -1.0, ALU.mult, l2[:, cols(t)], ALU.min)
-        b_step(0)
-        p_step(TILES - 1)
-        ln_q(0)
-        ln_q(1)
-        square(0)
-        square(1)
-        ln_q(2)
-        square(2)
-        ln_q(3)
-        for t in range(TILES - 1):
-            b_step(t + 1)
-            a_step(t)
+            if t * N < POOL_COLS:
+                p_step(nc.gpsimd, t * N, min((t + 1) * N, POOL_COLS))
+        p_step(nc.vector, POOL_COLS, (TILES - 1) * N)
+        p_step(nc.vector, (TILES - 1) * N, TILES * N)
+        for t in range(TILES):
+            act(lnq[:, cols(t)], prod[:, cols(t)], ACT.Ln, scale=gain[:, t : t + 1], bias=1.0)
+        for t in range(TILES):
+            t2_step(t)
+        for t in range(TILES):
+            t1_step(t)
 
         for t in range(TILES):
             act(rq[:, cols(t)], lnq[:, cols(t)], ACT.Exp, scale=-1.0)
-            if t == 1:
-                square(3)
 
-        def br_step(t):
-            tt(bb[:, cols(t)], bb[:, cols(t)], rq[:, cols(t)], ALU.mult)
+        def r_step(t):
+            stt(t2[:, cols(t)], t2[:, cols(t)], gain[:, t : t + 1], ALU.mult, rq[:, cols(t)], ALU.mult)
 
         def w_step(t):
-            tt(ww[:, cols(t)], bb[:, cols(t)], aa[:, cols(t)], ALU.subtract)
+            tt(ww[:, cols(t)], t2[:, cols(t)], t1[:, cols(t)], ALU.subtract)
 
         def cw_step(t):
-            tt(ww[:, cols(t)], c0[t][:], ww[:, cols(t)], ALU.mult)
+            tt(ww[:, cols(t)], cs[:, cols(t)], ww[:, cols(t)], ALU.mult)
 
         def y_step(t):
             g, h = divmod(t, HALVES)
@@ -215,8 +198,6 @@ def tile_rows_bsoftprod_kernel(tc, x, w1_words, w1_scales, w2_words, w2_scales, 
             nc.sync.dma_start(out=out[g, h * P : (h + 1) * P, :], in_=yy[:, cols(t)])
 
         for pair in ((0, 1), (2, 3)):
-            if pair[0] == 2:
-                a_step(3)
-            for step in (br_step, w_step, cw_step, y_step):
+            for step in (r_step, w_step, cw_step, y_step):
                 for t in pair:
                     step(t)

@@ -1,3 +1,4 @@
+import math
 from contextlib import ExitStack
 
 import concourse.mybir as mybir
@@ -21,6 +22,7 @@ TILES = G * HALVES
 CHUNKS = 2
 CW = N // CHUNKS
 POOL_COLS = 2 * N + 192
+POOL_TAIL = 320
 TINY = 2.0**-60
 FLOPS = 3 * 2 * G * D * M * N
 
@@ -121,7 +123,7 @@ def tile_rows_bsoftprod_kernel(tc, x, w1_words, w1_scales, w2_words, w2_scales, 
             z1.append(product("w1", x_codes, x_scales, t, 2 * h))
             z2.append(product("w2", x_codes, x_scales, t, 2 * h + 1))
 
-        m1, m2, z2_sb, diff, sd, cs = (wide(n) for n in ("m1", "m2", "z2_sb", "diff", "sd", "cs"))
+        m1, m2, z2_sb, diff, th, cs = (wide(n) for n in ("m1", "m2", "z2_sb", "diff", "th", "cs"))
         l1, l2, s1, s2, prod, lnq = (wide(n) for n in ("l1", "l2", "s1", "s2", "prod", "lnq"))
         t1, t2, rq, ww, yy = (wide(n) for n in ("t1", "t2", "rq", "ww", "yy"))
 
@@ -148,26 +150,28 @@ def tile_rows_bsoftprod_kernel(tc, x, w1_words, w1_scales, w2_words, w2_scales, 
             else:
                 d_step(t - 1)
         d_step(TILES - 1)
-        c0 = [product("wo", dy_codes, dy_scales, t, 2 * (t % HALVES) + 1) for t in range(TILES)]
-        z2 = []
-        for t in range(TILES):
-            act(sd[:, cols(t)], diff[:, cols(t)], ACT.Sigmoid)
-            tt(cs[:, cols(t)], c0[t][:], sd[:, cols(t)], ALU.mult)
-            z2.append(product("w2", x_codes, x_scales, t, 2 * (t % HALVES) + 1))
+
+        def tanh_d(t):
+            act(th[:, cols(t)], diff[:, cols(t)], ACT.Tanh, scale=0.5)
+
+        def cs_step(t):
+            stt(cs[:, cols(t)], th[:, cols(t)], 1.0, ALU.add, c0[t][:], ALU.mult)
+
+        c0 = [product("wo", dy_codes, dy_scales, t, 2 * t + 1) for t in range(HALVES)]
+        for t in range(HALVES):
+            tanh_d(t)
+            cs_step(t)
+            z2[t] = product("w2", x_codes, x_scales, t, 2 * t + 1)
 
         def p_step(engine, lo, hi):
             engine.tensor_tensor(out=prod[:, lo:hi], in0=s1[:, lo:hi], in1=s2[:, lo:hi], op=ALU.mult)
-
-        def t2_step(t):
-            stt(t2[:, cols(t)], m1[:, cols(t)], 1.0, ALU.subtract, s2[:, cols(t)], ALU.mult)
-
-        def t1_step(t):
-            stt(t1[:, cols(t)], sd[:, cols(t)], 1.0, ALU.subtract, lnq[:, cols(t)], ALU.mult)
 
         for t in range(TILES):
             act(l1[:, cols(t)], m1[:, cols(t)], ACT.Ln, bias=TINY)
             act(l2[:, cols(t)], m2[:, cols(t)], ACT.Ln, bias=TINY)
             stt(s1[:, cols(t)], z1[t][:], -1.0, ALU.mult, l1[:, cols(t)], ALU.min)
+            if t >= HALVES:
+                c0.append(product("wo", dy_codes, dy_scales, t, 2 * (t - HALVES)))
             stt(s2[:, cols(t)], z2[t][:], -1.0, ALU.mult, l2[:, cols(t)], ALU.min)
             if t * N < POOL_COLS:
                 p_step(nc.gpsimd, t * N, min((t + 1) * N, POOL_COLS))
@@ -175,29 +179,50 @@ def tile_rows_bsoftprod_kernel(tc, x, w1_words, w1_scales, w2_words, w2_scales, 
         p_step(nc.vector, (TILES - 1) * N, TILES * N)
         for t in range(TILES):
             act(lnq[:, cols(t)], prod[:, cols(t)], ACT.Ln, scale=gain[:, t : t + 1], bias=1.0)
-        for t in range(TILES):
-            t2_step(t)
-        for t in range(TILES):
-            t1_step(t)
+        stt(t2[:], m1[:], 1.0, ALU.subtract, s2[:], ALU.mult)
 
-        for t in range(TILES):
-            act(rq[:, cols(t)], lnq[:, cols(t)], ACT.Exp, scale=-1.0)
+        def pair_cols(g):
+            return slice(g * HALVES * N, (g + 1) * HALVES * N)
+
+        def t1_step(g):
+            stt(t1[:, pair_cols(g)], th[:, pair_cols(g)], 1.0, ALU.subtract, lnq[:, pair_cols(g)], ALU.mult)
+
+        t1_step(0)
+
+        def recip_q(t):
+            act(rq[:, cols(t)], lnq[:, cols(t)], ACT.Exp, scale=-1.0, bias=-math.log(2.0))
 
         def r_step(t):
             stt(t2[:, cols(t)], t2[:, cols(t)], gain[:, t : t + 1], ALU.mult, rq[:, cols(t)], ALU.mult)
 
         def w_step(t):
-            tt(ww[:, cols(t)], t2[:, cols(t)], t1[:, cols(t)], ALU.subtract)
+            stt(ww[:, cols(t)], t1[:, cols(t)], -0.25, ALU.mult, t2[:, cols(t)], ALU.add)
 
-        def cw_step(t):
-            tt(ww[:, cols(t)], cs[:, cols(t)], ww[:, cols(t)], ALU.mult)
+        def cw_step(engine, lo, hi):
+            engine.tensor_tensor(out=ww[:, lo:hi], in0=cs[:, lo:hi], in1=ww[:, lo:hi], op=ALU.mult)
 
-        def y_step(t):
+        def y_step(t, lo, hi):
             g, h = divmod(t, HALVES)
-            tt(yy[:, cols(t)], ww[:, cols(t)], old_sb[:, cols(t)], ALU.add)
-            nc.sync.dma_start(out=out[g, h * P : (h + 1) * P, :], in_=yy[:, cols(t)])
+            part = slice(t * N + lo, t * N + hi)
+            tt(yy[:, part], ww[:, part], old_sb[:, part], ALU.add)
+            nc.sync.dma_start(out=out[g, h * P : (h + 1) * P, lo:hi], in_=yy[:, part])
 
-        for pair in ((0, 1), (2, 3)):
-            for step in (r_step, w_step, cw_step, y_step):
-                for t in pair:
-                    step(t)
+        for step in (recip_q, r_step, w_step):
+            for t in (0, 1):
+                step(t)
+        cw_step(nc.gpsimd, 2 * N - POOL_TAIL, 2 * N)
+        for step in (tanh_d, cs_step, recip_q):
+            for t in (2, 3):
+                step(t)
+        cw_step(nc.vector, 0, 2 * N - POOL_TAIL)
+        t1_step(1)
+        y_step(0, 0, N)
+        y_step(1, 0, N)
+        for step in (r_step, w_step):
+            for t in (2, 3):
+                step(t)
+        cw_step(nc.vector, 2 * N, 3 * N)
+        cw_step(nc.vector, 3 * N, 4 * N)
+        y_step(2, 0, N)
+        y_step(3, 0, N // 2)
+        y_step(3, N // 2, N)

@@ -21,7 +21,7 @@ HALVES = M // P
 TILES = G * HALVES
 CHUNKS = 2
 CW = N // CHUNKS
-POOL_COLS = 2 * N + 192
+POOL_COLS = 2 * N + 288
 POOL_TAIL = 320
 TINY = 2.0**-60
 FLOPS = 3 * 2 * G * D * M * N
@@ -123,7 +123,7 @@ def tile_rows_bsoftprod_kernel(tc, x, w1_words, w1_scales, w2_words, w2_scales, 
             z1.append(product("w1", x_codes, x_scales, t, 2 * h))
             z2.append(product("w2", x_codes, x_scales, t, 2 * h + 1))
 
-        m1, m2, z2_sb, diff, th, cs = (wide(n) for n in ("m1", "m2", "z2_sb", "diff", "th", "cs"))
+        m1, m2, z1_sb, diff, th, cs = (wide(n) for n in ("m1", "m2", "z1_sb", "diff", "th", "cs"))
         l1, l2, s1, s2, prod, lnq = (wide(n) for n in ("l1", "l2", "s1", "s2", "prod", "lnq"))
         t1, t2, rq, ww, yy = (wide(n) for n in ("t1", "t2", "rq", "ww", "yy"))
 
@@ -137,44 +137,48 @@ def tile_rows_bsoftprod_kernel(tc, x, w1_words, w1_scales, w2_words, w2_scales, 
             nc.vector.tensor_tensor(out=dst, in0=in0, in1=in1, op=op)
 
         def d_step(t):
-            tt(diff[:, cols(t)], z1[t][:], z2_sb[:, cols(t)], ALU.subtract)
+            tt(diff[:, cols(t)], z2[t][:], z1_sb[:, cols(t)], ALU.subtract)
 
         quantize(dy_codes, dy_scales, interleave("dy", dy_raw[0], 0), 0)
-        dy_last = interleave("dy", dy_raw[1], 1)
+        dy_last = sb.tile([P, CW, PACK], BF16, name="dy_bf1", align_bytes=64)
+        nc.gpsimd.tensor_scalar(
+            out=dy_last[:], in0=dy_raw[1][:].rearrange("p j n -> p n j"), scalar1=1.0, scalar2=0.0, op0=ALU.mult, op1=ALU.add
+        )
         for t in range(TILES):
             act(m1[:, cols(t)], z1[t][:], ACT.Sigmoid, scale=-1.0)
+            nc.vector.tensor_copy(out=z1_sb[:, cols(t)], in_=z1[t][:])
             act(m2[:, cols(t)], z2[t][:], ACT.Sigmoid, scale=-1.0)
-            nc.vector.tensor_copy(out=z2_sb[:, cols(t)], in_=z2[t][:])
-            if t == 0:
+            if t == TILES - 1:
                 quantize(dy_codes, dy_scales, dy_last, 1)
-            else:
+            if t >= 1:
                 d_step(t - 1)
         d_step(TILES - 1)
 
         def tanh_d(t):
-            act(th[:, cols(t)], diff[:, cols(t)], ACT.Tanh, scale=0.5)
+            act(th[:, cols(t)], diff[:, cols(t)], ACT.Tanh, scale=-0.5)
 
         def cs_step(t):
             stt(cs[:, cols(t)], th[:, cols(t)], 1.0, ALU.add, c0[t][:], ALU.mult)
 
-        c0 = [product("wo", dy_codes, dy_scales, t, 2 * t + 1) for t in range(HALVES)]
+        c0 = [product("wo", dy_codes, dy_scales, t, 2 * t) for t in range(HALVES)]
         for t in range(HALVES):
             tanh_d(t)
             cs_step(t)
-            z2[t] = product("w2", x_codes, x_scales, t, 2 * t + 1)
+            z1[t] = product("w1", x_codes, x_scales, t, 2 * t)
 
         def p_step(engine, lo, hi):
             engine.tensor_tensor(out=prod[:, lo:hi], in0=s1[:, lo:hi], in1=s2[:, lo:hi], op=ALU.mult)
 
-        for t in range(TILES):
-            act(l1[:, cols(t)], m1[:, cols(t)], ACT.Ln, bias=TINY)
-            act(l2[:, cols(t)], m2[:, cols(t)], ACT.Ln, bias=TINY)
-            stt(s1[:, cols(t)], z1[t][:], -1.0, ALU.mult, l1[:, cols(t)], ALU.min)
+        for t, lo, hi in [(0, 0, N // 2), (0, N // 2, N)] + [(t, 0, N) for t in range(1, TILES)]:
+            part = slice(t * N + lo, t * N + hi)
+            act(l2[:, part], m2[:, part], ACT.Ln, bias=TINY)
+            act(l1[:, part], m1[:, part], ACT.Ln, bias=TINY)
+            stt(s2[:, part], z2[t][:, lo:hi], -1.0, ALU.mult, l2[:, part], ALU.min)
+            stt(s1[:, part], z1[t][:, lo:hi], -1.0, ALU.mult, l1[:, part], ALU.min)
             if t >= HALVES:
                 c0.append(product("wo", dy_codes, dy_scales, t, 2 * (t - HALVES)))
-            stt(s2[:, cols(t)], z2[t][:], -1.0, ALU.mult, l2[:, cols(t)], ALU.min)
-            if t * N < POOL_COLS:
-                p_step(nc.gpsimd, t * N, min((t + 1) * N, POOL_COLS))
+            if part.start < POOL_COLS:
+                p_step(nc.gpsimd, part.start, min(part.stop, POOL_COLS))
         p_step(nc.vector, POOL_COLS, (TILES - 1) * N)
         p_step(nc.vector, (TILES - 1) * N, TILES * N)
         for t in range(TILES):

@@ -118,10 +118,14 @@ def tile_rows_bsoftprod_kernel(tc, x, w1_words, w1_scales, w2_words, w2_scales, 
             quantize(x_codes, x_scales, interleave("x", x_raw[c], c), c)
 
         z1, z2 = [], []
-        for t in range(TILES):
+
+        def forward(t):
             h = t % HALVES
             z1.append(product("w1", x_codes, x_scales, t, 2 * h))
             z2.append(product("w2", x_codes, x_scales, t, 2 * h + 1))
+
+        for t in range(TILES - 1):
+            forward(t)
 
         m1, m2, z1_sb, diff, th, cs = (wide(n) for n in ("m1", "m2", "z1_sb", "diff", "th", "cs"))
         l1, l2, s1, s2, prod, lnq = (wide(n) for n in ("l1", "l2", "s1", "s2", "prod", "lnq"))
@@ -140,19 +144,7 @@ def tile_rows_bsoftprod_kernel(tc, x, w1_words, w1_scales, w2_words, w2_scales, 
             tt(diff[:, cols(t)], z2[t][:], z1_sb[:, cols(t)], ALU.subtract)
 
         quantize(dy_codes, dy_scales, interleave("dy", dy_raw[0], 0), 0)
-        dy_last = sb.tile([P, CW, PACK], BF16, name="dy_bf1", align_bytes=64)
-        nc.gpsimd.tensor_scalar(
-            out=dy_last[:], in0=dy_raw[1][:].rearrange("p j n -> p n j"), scalar1=1.0, scalar2=0.0, op0=ALU.mult, op1=ALU.add
-        )
-        for t in range(TILES):
-            act(m1[:, cols(t)], z1[t][:], ACT.Sigmoid, scale=-1.0)
-            nc.vector.tensor_copy(out=z1_sb[:, cols(t)], in_=z1[t][:])
-            act(m2[:, cols(t)], z2[t][:], ACT.Sigmoid, scale=-1.0)
-            if t == TILES - 1:
-                quantize(dy_codes, dy_scales, dy_last, 1)
-            if t >= 1:
-                d_step(t - 1)
-        d_step(TILES - 1)
+        dy_last = interleave("dy", dy_raw[1], 1)
 
         def tanh_d(t):
             act(th[:, cols(t)], diff[:, cols(t)], ACT.Tanh, scale=-0.5)
@@ -160,11 +152,37 @@ def tile_rows_bsoftprod_kernel(tc, x, w1_words, w1_scales, w2_words, w2_scales, 
         def cs_step(t):
             stt(cs[:, cols(t)], th[:, cols(t)], 1.0, ALU.add, c0[t][:], ALU.mult)
 
-        c0 = [product("wo", dy_codes, dy_scales, t, 2 * t) for t in range(HALVES)]
-        for t in range(HALVES):
-            tanh_d(t)
-            cs_step(t)
-            z1[t] = product("w1", x_codes, x_scales, t, 2 * t)
+        def one_minus(dst, src):
+            nc.gpsimd.tensor_scalar(out=dst, in0=src, scalar1=-1.0, scalar2=1.0, op0=ALU.mult, op1=ALU.add)
+
+        def sigmoids(t):
+            act(m1[:, cols(t)], z1[t][:], ACT.Sigmoid, scale=-1.0)
+            nc.vector.tensor_copy(out=z1_sb[:, cols(t)], in_=z1[t][:])
+            act(m2[:, cols(t)], z2[t][:], ACT.Sigmoid, scale=-1.0)
+
+        first = cols(0)
+        sigmoids(0)
+        quantize(dy_codes, dy_scales, dy_last, 1)
+        d_step(0)
+        one_minus(z1_sb[:, first], m1[:, first])
+        sigmoids(1)
+        sigmoids(2)
+        c0 = [product("wo", dy_codes, dy_scales, 0, 0)]
+        forward(3)
+        c0.append(product("wo", dy_codes, dy_scales, 1, 2))
+        tanh_d(0)
+        d_step(1)
+        cs_step(0)
+        z1[0] = product("w1", x_codes, x_scales, 0, 0)
+        one_minus(t1[:, first], th[:, first])
+        nc.gpsimd.tensor_tensor(out=t2[:, first], in0=z1_sb[:, first], in1=cs[:, first], op=ALU.mult)
+        nc.gpsimd.tensor_tensor(out=t1[:, first], in0=t1[:, first], in1=cs[:, first], op=ALU.mult)
+        sigmoids(3)
+        tanh_d(1)
+        d_step(2)
+        cs_step(1)
+        z1[1] = product("w1", x_codes, x_scales, 1, 2)
+        d_step(3)
 
         def p_step(engine, lo, hi):
             engine.tensor_tensor(out=prod[:, lo:hi], in0=s1[:, lo:hi], in1=s2[:, lo:hi], op=ALU.mult)
@@ -183,15 +201,15 @@ def tile_rows_bsoftprod_kernel(tc, x, w1_words, w1_scales, w2_words, w2_scales, 
         p_step(nc.vector, (TILES - 1) * N, TILES * N)
         for t in range(TILES):
             act(lnq[:, cols(t)], prod[:, cols(t)], ACT.Ln, scale=gain[:, t : t + 1], bias=1.0)
-        stt(t2[:], m1[:], 1.0, ALU.subtract, s2[:], ALU.mult)
+        stt(ww[:, first], t1[:, first], 0.25, ALU.mult, lnq[:, first], ALU.mult)
+        stt(t2[:, first], t2[:, first], gain[:, 0:1], ALU.mult, s2[:, first], ALU.mult)
+        tt(ww[:, first], ww[:, first], old_sb[:, first], ALU.add)
+        stt(t2[:, N:], m1[:, N:], 1.0, ALU.subtract, s2[:, N:], ALU.mult)
 
-        def pair_cols(g):
-            return slice(g * HALVES * N, (g + 1) * HALVES * N)
+        def t1_step(lo, hi):
+            stt(t1[:, lo:hi], th[:, lo:hi], 1.0, ALU.subtract, lnq[:, lo:hi], ALU.mult)
 
-        def t1_step(g):
-            stt(t1[:, pair_cols(g)], th[:, pair_cols(g)], 1.0, ALU.subtract, lnq[:, pair_cols(g)], ALU.mult)
-
-        t1_step(0)
+        t1_step(N, 2 * N)
 
         def recip_q(t):
             act(rq[:, cols(t)], lnq[:, cols(t)], ACT.Exp, scale=-1.0, bias=-math.log(2.0))
@@ -211,16 +229,19 @@ def tile_rows_bsoftprod_kernel(tc, x, w1_words, w1_scales, w2_words, w2_scales, 
             tt(yy[:, part], ww[:, part], old_sb[:, part], ALU.add)
             nc.sync.dma_start(out=out[g, h * P : (h + 1) * P, lo:hi], in_=yy[:, part])
 
-        for step in (recip_q, r_step, w_step):
-            for t in (0, 1):
-                step(t)
+        recip_q(1)
+        recip_q(0)
+        r_step(1)
+        tt(t2[:, first], t2[:, first], rq[:, first], ALU.mult)
+        w_step(1)
         cw_step(nc.gpsimd, 2 * N - POOL_TAIL, 2 * N)
         for step in (tanh_d, cs_step, recip_q):
             for t in (2, 3):
                 step(t)
-        cw_step(nc.vector, 0, 2 * N - POOL_TAIL)
-        t1_step(1)
-        y_step(0, 0, N)
+        tt(yy[:, first], ww[:, first], t2[:, first], ALU.subtract)
+        nc.sync.dma_start(out=out[0, 0:P, :], in_=yy[:, first])
+        cw_step(nc.vector, N, 2 * N - POOL_TAIL)
+        t1_step(2 * N, 4 * N)
         y_step(1, 0, N)
         for step in (r_step, w_step):
             for t in (2, 3):

import math
from contextlib import ExitStack

import concourse.mybir as mybir

F32 = mybir.dt.float32
BF16 = mybir.dt.bfloat16
I32 = mybir.dt.int32
U32 = mybir.dt.uint32
U8 = mybir.dt.uint8
FP8X4 = mybir.dt.float8_e4m3fn_x4
FP4X4 = mybir.dt.float4_e2m1fn_x4
ACT = mybir.ActivationFunctionType
ALU = mybir.AluOpType

G, D, M, N = 2, 256, 256, 512
P = 128
PACK = 4
ROWS = D // PACK
HALVES = M // P
TILES = G * HALVES
CHUNKS = 2
CW = N // CHUNKS
POOL_COLS = 2 * N + 288
POOL_TAIL = 320
TINY = 2.0**-60
FLOPS = 3 * 2 * G * D * M * N


def tile_rows_bsoftprod_kernel(tc, x, w1_words, w1_scales, w2_words, w2_scales, gn, wo_words, wo_scales, dy, old, out):
    nc = tc.nc
    with ExitStack() as ctx:
        sb = ctx.enter_context(tc.tile_pool(name="sb", bufs=1))
        ps = ctx.enter_context(tc.psum_pool(name="ps", bufs=1))
        ctx.enter_context(tc.manual_schedule())

        def cols(t):
            return slice(t * N, (t + 1) * N)

        def wide(name):
            return sb.tile([P, TILES * N], F32, name=name, align_bytes=64)

        words = {}
        planes = {}
        for name in ("w1", "w2", "wo"):
            words[name] = sb.tile([P, 2 * M], U8, name=name + "_words", align_bytes=64)
            planes[name] = sb.tile([P, M], U8, name=name + "_plane", align_bytes=64)
            engine = nc.vector if name == "wo" else nc.gpsimd
            engine.memset(planes[name][:].bitcast(U32), 0)

        def load_words(name, src):
            nc.sync.dma_start(out=words[name][:].bitcast(I32), in_=src.rearrange("g p b -> (g p) b").bitcast(I32))

        def load_plane(name, src, q, queue):
            rows = src.rearrange("g f m -> (g f) m")
            queue.dma_start(out=planes[name][32 * q : 32 * q + 4, :].bitcast(I32), in_=rows[4 * q : 4 * q + 4, :].bitcast(I32))

        def load_raw(name, src, c):
            raw = sb.tile([P, PACK, CW], F32, name="%s_raw%d" % (name, c), align_bytes=64)
            nc.sync.dma_start(out=raw[:], in_=src.rearrange("g (p j) n -> (g p) j n", j=PACK)[:, :, c * CW : (c + 1) * CW])
            return raw

        def interleave(name, raw, c):
            grouped = sb.tile([P, CW, PACK], BF16, name="%s_bf%d" % (name, c), align_bytes=64)
            nc.vector.tensor_copy(
                out=grouped[:].rearrange("p (c i) j -> p c j i", i=4),
                in_=raw[:].rearrange("p j (c i) -> p c j i", i=4),
            )
            return grouped

        def quantize(codes, scales, grouped, c):
            window = slice(c * CW, (c + 1) * CW)
            nc.vector.quantize_mx(
                out=codes[:, window].bitcast(FP8X4),
                scales=scales[:, window],
                in_=grouped[:].rearrange("p n j -> p (n j)"),
            )

        def product(name, codes, scales, t, slot):
            g, h = divmod(t, HALVES)
            rows = slice(g * ROWS, (g + 1) * ROWS)
            bank = ps.tile([P, N], F32, name="bank%d_%d" % (g, slot))
            nc.tensor.matmul_mx(
                out=bank[:],
                lhsT=words[name][rows, 2 * P * h : 2 * P * (h + 1)].bitcast(FP4X4),
                lhsT_scale=planes[name][rows, P * h : P * (h + 1)],
                rhs=codes[rows, :].bitcast(FP8X4),
                rhs_scale=scales[rows, :],
                start=True,
                stop=True,
            )
            return bank

        x_raw = [load_raw("x", x, c) for c in range(CHUNKS)]
        weights = (("w1", w1_words, w1_scales), ("w2", w2_words, w2_scales))
        for name, src_words, src_scales in weights:
            load_words(name, src_words)
            for q in (0, 1):
                load_plane(name, src_scales, q, nc.sync)
        for name, src_words, src_scales in weights:
            for q in (2, 3):
                load_plane(name, src_scales, q, nc.gpsimd)
        dy_raw = [load_raw("dy", dy, c) for c in range(CHUNKS)]
        load_words("wo", wo_words)
        for q in range(4):
            load_plane("wo", wo_scales, q, nc.sync)
        gain = sb.tile([P, TILES], F32, name="gain")
        with nc.allow_non_contiguous_dma(reason="one gain a partition"):
            nc.sync.dma_start(out=gain[:], in_=gn.rearrange("g (h p) o -> p (g h o)", p=P))
        old_sb = wide("old_sb")
        nc.sync.dma_start(out=old_sb[:].rearrange("p (t n) -> p t n", n=N), in_=old.rearrange("g (h p) n -> p (g h) n", p=P))

        x_codes = sb.tile([P, N], U32, name="x_codes", align_bytes=64)
        x_scales = sb.tile([P, N], U8, name="x_scales", align_bytes=64)
        dy_codes = sb.tile([P, N], U32, name="dy_codes", align_bytes=64)
        dy_scales = sb.tile([P, N], U8, name="dy_scales", align_bytes=64)
        for c in range(CHUNKS):
            quantize(x_codes, x_scales, interleave("x", x_raw[c], c), c)

        z1, z2 = [], []

        def forward(t):
            h = t % HALVES
            z1.append(product("w1", x_codes, x_scales, t, 2 * h))
            z2.append(product("w2", x_codes, x_scales, t, 2 * h + 1))

        for t in range(TILES - 1):
            forward(t)

        m1, m2, z1_sb, diff, th, cs = (wide(n) for n in ("m1", "m2", "z1_sb", "diff", "th", "cs"))
        l1, l2, s1, s2, prod, lnq = (wide(n) for n in ("l1", "l2", "s1", "s2", "prod", "lnq"))
        t1, t2, rq, ww, yy = (wide(n) for n in ("t1", "t2", "rq", "ww", "yy"))

        def act(dst, src, func, **kw):
            nc.scalar.activation(out=dst, in_=src, func=func, **kw)

        def stt(dst, in0, scalar, op0, in1, op1):
            nc.vector.scalar_tensor_tensor(out=dst, in0=in0, scalar=scalar, in1=in1, op0=op0, op1=op1)

        def tt(dst, in0, in1, op):
            nc.vector.tensor_tensor(out=dst, in0=in0, in1=in1, op=op)

        def d_step(t):
            tt(diff[:, cols(t)], z2[t][:], z1_sb[:, cols(t)], ALU.subtract)

        quantize(dy_codes, dy_scales, interleave("dy", dy_raw[0], 0), 0)
        dy_last = interleave("dy", dy_raw[1], 1)

        def tanh_d(t):
            act(th[:, cols(t)], diff[:, cols(t)], ACT.Tanh, scale=-0.5)

        def cs_step(t):
            stt(cs[:, cols(t)], th[:, cols(t)], 1.0, ALU.add, c0[t][:], ALU.mult)

        def one_minus(dst, src):
            nc.gpsimd.tensor_scalar(out=dst, in0=src, scalar1=-1.0, scalar2=1.0, op0=ALU.mult, op1=ALU.add)

        def sigmoids(t):
            act(m1[:, cols(t)], z1[t][:], ACT.Sigmoid, scale=-1.0)
            nc.vector.tensor_copy(out=z1_sb[:, cols(t)], in_=z1[t][:])
            act(m2[:, cols(t)], z2[t][:], ACT.Sigmoid, scale=-1.0)

        first = cols(0)
        sigmoids(0)
        quantize(dy_codes, dy_scales, dy_last, 1)
        d_step(0)
        one_minus(z1_sb[:, first], m1[:, first])
        sigmoids(1)
        sigmoids(2)
        c0 = [product("wo", dy_codes, dy_scales, 0, 0)]
        forward(3)
        c0.append(product("wo", dy_codes, dy_scales, 1, 2))
        tanh_d(0)
        d_step(1)
        cs_step(0)
        z1[0] = product("w1", x_codes, x_scales, 0, 0)
        one_minus(t1[:, first], th[:, first])
        nc.gpsimd.tensor_tensor(out=t2[:, first], in0=z1_sb[:, first], in1=cs[:, first], op=ALU.mult)
        nc.gpsimd.tensor_tensor(out=t1[:, first], in0=t1[:, first], in1=cs[:, first], op=ALU.mult)
        sigmoids(3)
        tanh_d(1)
        d_step(2)
        cs_step(1)
        z1[1] = product("w1", x_codes, x_scales, 1, 2)
        d_step(3)

        def p_step(engine, lo, hi):
            engine.tensor_tensor(out=prod[:, lo:hi], in0=s1[:, lo:hi], in1=s2[:, lo:hi], op=ALU.mult)

        for t, lo, hi in [(0, 0, N // 2), (0, N // 2, N)] + [(t, 0, N) for t in range(1, TILES)]:
            part = slice(t * N + lo, t * N + hi)
            act(l2[:, part], m2[:, part], ACT.Ln, bias=TINY)
            act(l1[:, part], m1[:, part], ACT.Ln, bias=TINY)
            stt(s2[:, part], z2[t][:, lo:hi], -1.0, ALU.mult, l2[:, part], ALU.min)
            stt(s1[:, part], z1[t][:, lo:hi], -1.0, ALU.mult, l1[:, part], ALU.min)
            if t >= HALVES:
                c0.append(product("wo", dy_codes, dy_scales, t, 2 * (t - HALVES)))
            if part.start < POOL_COLS:
                p_step(nc.gpsimd, part.start, min(part.stop, POOL_COLS))
        p_step(nc.vector, POOL_COLS, (TILES - 1) * N)
        p_step(nc.vector, (TILES - 1) * N, TILES * N)
        for t in range(TILES):
            act(lnq[:, cols(t)], prod[:, cols(t)], ACT.Ln, scale=gain[:, t : t + 1], bias=1.0)
        stt(ww[:, first], t1[:, first], 0.25, ALU.mult, lnq[:, first], ALU.mult)
        stt(t2[:, first], t2[:, first], gain[:, 0:1], ALU.mult, s2[:, first], ALU.mult)
        tt(ww[:, first], ww[:, first], old_sb[:, first], ALU.add)
        stt(t2[:, N:], m1[:, N:], 1.0, ALU.subtract, s2[:, N:], ALU.mult)

        def t1_step(lo, hi):
            stt(t1[:, lo:hi], th[:, lo:hi], 1.0, ALU.subtract, lnq[:, lo:hi], ALU.mult)

        t1_step(N, 2 * N)

        def recip_q(t):
            act(rq[:, cols(t)], lnq[:, cols(t)], ACT.Exp, scale=-1.0, bias=-math.log(2.0))

        def r_step(t):
            stt(t2[:, cols(t)], t2[:, cols(t)], gain[:, t : t + 1], ALU.mult, rq[:, cols(t)], ALU.mult)

        def w_step(t):
            stt(ww[:, cols(t)], t1[:, cols(t)], -0.25, ALU.mult, t2[:, cols(t)], ALU.add)

        def cw_step(engine, lo, hi):
            engine.tensor_tensor(out=ww[:, lo:hi], in0=cs[:, lo:hi], in1=ww[:, lo:hi], op=ALU.mult)

        def y_step(t, lo, hi):
            g, h = divmod(t, HALVES)
            part = slice(t * N + lo, t * N + hi)
            tt(yy[:, part], ww[:, part], old_sb[:, part], ALU.add)
            nc.sync.dma_start(out=out[g, h * P : (h + 1) * P, lo:hi], in_=yy[:, part])

        recip_q(1)
        recip_q(0)
        r_step(1)
        tt(t2[:, first], t2[:, first], rq[:, first], ALU.mult)
        w_step(1)
        cw_step(nc.gpsimd, 2 * N - POOL_TAIL, 2 * N)
        for step in (tanh_d, cs_step, recip_q):
            for t in (2, 3):
                step(t)
        tt(yy[:, first], ww[:, first], t2[:, first], ALU.subtract)
        nc.sync.dma_start(out=out[0, 0:P, :], in_=yy[:, first])
        cw_step(nc.vector, N, 2 * N - POOL_TAIL)
        t1_step(2 * N, 4 * N)
        y_step(1, 0, N)
        for step in (r_step, w_step):
            for t in (2, 3):
                step(t)
        cw_step(nc.vector, 2 * N, 3 * N)
        cw_step(nc.vector, 3 * N, 4 * N)
        y_step(2, 0, N)
        y_step(3, 0, N // 2)
        y_step(3, N // 2, N)
